import numpy as np, ml_dtypes
CORES = [1,3,5,9,11,13]
N = 6
import mx_ref
NC, KT, WT = 128, 4, 5
BF = ml_dtypes.bfloat16
def cut(t, i, w=512):
    return t[:, w * i:w * i + w]
def pk(c, s, i=0):
    return (np.ascontiguousarray(c[:, 512 * i:512 * i + 512]), mx_ref.live(s[:, 128 * i:128 * i + 128]))
def inputs(rng, e, E):
    def f(*shape):
        v = (rng.standard_normal(shape, dtype=np.float32) * np.exp2(rng.integers(-2, 3, shape[:-1] + (1,)))).astype(BF)
        return mx_ref.spread((v.astype(np.float32) * np.exp2(rng.integers(-E, E + 1, shape[:-2] + (1, 1))).astype(np.float32)).astype(BF), rng, e)
    def packed(k):
        c = np.zeros((N, 128, k * 512), np.uint8); s = np.zeros((N, 128, k * 128), np.uint8)
        for r in range(N):
            for i in range(k):
                a, b = mx_ref.quantize(f(128, 512)); c[r][:, 512 * i:512 * i + 512] = a; s[r][:, 128 * i:128 * i + 128] = mx_ref.plane(b, rng)
        return c, s
    d = {}
    d["wc"], d["ws"] = packed(KT * WT)
    d["x"] = f(N, 128, KT * 4 * NC)
    return d
def setup_inputs(rng):
    return inputs(rng, 0, 0)
def setup_inputs_blocks(rng):
    return inputs(rng, 2, 0)
def setup_inputs_wide(rng):
    d = inputs(rng, 0, 1); d["x"] = inputs(rng, 0, 0)["x"]
    return d
def reference(wc, ws, x):
    X = [[mx_ref.quantize(cut(x[j], t, 4 * NC)) for t in range(KT)] for j in range(N)]
    y = np.zeros((N, 128, N * WT * NC), np.float32)
    for r in range(N):
        for b in range(N * WT):
            j, i = divmod(b, WT)
            for t in range(KT):
                p = mx_ref.matmul(pk(wc[r], ws[r], KT * i + t), X[j][t])
                z = p if t == 0 else z + p
            y[r][:, NC * b:NC * b + NC] = z
    return {"y": y}

@@ -1,0 +1,240 @@
+from concourse.bass import DstId, RemoteDMATransfer
+from concourse.mybir import dt, ActivationFunctionType
+
+KT, WT = 4, 5
+NCORES = 16
+R = 4
+S = 4
+GR = 3
+GW = GR * 128
+PAIRS = [(0, 1), (2, 3), (4,)]
+NST = 2 * GR * len(PAIRS)
+KE = 8
+CE = 8
+DE = 16
+
+SCRATCH = {
+    "xb": ("sbuf", [128, 512], "bfloat16"),
+    "g0": ("sbuf", [128, GW], "float8_e4m3fn_x4"),
+    "g1": ("sbuf", [128, GW], "float8_e4m3fn_x4"),
+    "p0": ("sbuf", [128, GW], "uint8"),
+    "p1": ("sbuf", [128, GW], "uint8"),
+    "wq": ("sbuf", [128, R * 128], "float8_e4m3fn_x4"),
+    "wp": ("sbuf", [128, R * 128], "uint8"),
+    "yst": ("sbuf", [128, S * 128], "float32"),
+    "ps": ("psum", [128, 8 * 512], "float32"),
+}
+SEMAPHORES = (["xl", "q", "mm", "evv", "evs", "lc", "lx"]
+              + ["wl%d" % s for s in range(R)]
+              + ["ys%d" % n for n in range(NST)]
+              + ["%s%d" % (a, t) for a in ("la", "aa", "ae", "ab", "ce") for t in range(KT)]
+              + ["fr0", "fr1"])
+
+
+def engines(mask):
+    return [1 << b for b in range(mask.bit_length()) if (mask >> b) & 1]
+
+
+def pick(mask, n, step=1):
+    e = engines(mask)[::step][:n]
+    return sum(e), len(e)
+
+
+def dst(topo, c):
+    rid, pid, _ = topo.addr(c)
+    return DstId(rid=rid, pnc=pid)
+
+
+def plan(T, topo):
+    out = {}
+    cores = list(T.cores)
+    for c in cores:
+        out.setdefault(topo.chip(c), {"ranks": []})["ranks"].append(c)
+    for ch, o in out.items():
+        helpers = [c for c in range(NCORES) if topo.chip(c) == ch and c not in cores]
+        far = [c for c in range(NCORES) if topo.mates(topo.chip(c), ch)]
+        o["mate"] = topo.chip(far[0])
+        dies = sorted(set(topo.die(c) for c in helpers), reverse=True)
+        a, b = [[c for c in helpers if topo.die(c) == d and topo.may_write(c, far[0])] for d in dies]
+        e, f = [[c for c in helpers if topo.die(c) == d and not topo.may_write(c, far[0])] for d in dies]
+        o["out"] = [a[0], b[0], b[-1], a[-1]]
+        o["in"] = [e[0], f[0], f[0], e[0]]
+    return out
+
+
+def transfer(topo, buf, cols, codes, to, mask, rsem):
+    v = buf[:, cols[0]:cols[1]]
+    if codes:
+        v = v.bitcast(dt.uint8)
+    return RemoteDMATransfer(dst_ids=[dst(topo, c) for c in to], dma_engine_mask=mask,
+                             remote_sem=rsem, srcs=[v], dsts=[v] * len(to))
+
+
+def rank_program(g, core, T, topo):
+    chips = plan(T, topo)
+    me = chips[topo.chip(core)]
+    far = chips[me["mate"]]
+    if T.rank_of(core) is None:
+        helper_program(g, core, T, topo, me, far)
+        return
+    grp, pln, sem = [T.g0, T.g1], [T.p0, T.p1], T.sem
+    mine = me["ranks"].index(core)
+    peers = [c for c in me["ranks"] if c != core]
+    own = (128 * mine, 128 * mine + 128)
+    km, kn = pick(topo.mask(core, peers[0]), KE, 2)
+
+    steps = [(p, t, i) for p in range(2) for t in range(KT) for i in range(WT)]
+    step_end = {}
+    last = {}
+    for k, (p, t, i) in enumerate(steps):
+        step_end[(p, t)] = k + 1
+        last[(p, i)] = k + 1
+
+    g.sync.dma_start(T.xb[:], T.x[:, 0:512]).then_inc(sem.xl, 16)
+    for k, (p, t, i) in enumerate(steps):
+        s = k % R
+        n = KT * i + t
+        if k >= R:
+            g.sync.wait_ge(sem.mm, k - R + 1)
+        w = T.wq[:, 128 * s:128 * s + 128].bitcast(dt.uint8)
+        g.sync.dma_start(w, T.wc[:, 512 * n:512 * n + 512]).then_inc(sem["wl%d" % s], 16)
+        g.sync.dma_start(T.wp[:, 128 * s:128 * s + 128], T.ws[:, 128 * n:128 * n + 128]).then_inc(sem["wl%d" % s], 16)
+
+    for t in range(1, KT):
+        g.scalar.wait_ge(sem.q, t)
+        g.scalar.dma_start(T.xb[:], T.x[:, 512 * t:512 * t + 512]).then_inc(sem.xl, 16)
+
+    for t in range(KT):
+        s = t % 2
+        if t >= 2:
+            g.vector.wait_ge(sem.mm, step_end[(0, t - 2)])
+            g.vector.wait_ge(sem["la%d" % (t - 2)], 2 * kn)
+        g.vector.wait_ge(sem.xl, 16 * (t + 1))
+        g.vector.quantize_mx(grp[s][:, own[0]:own[1]], pln[s][:, own[0]:own[1]], T.xb[:]).then_inc(sem.q, 1)
+
+    ones = engines(km)
+    for t in range(KT):
+        s = t % 2
+        if t >= 2:
+            g.wait_ge(sem.mm, step_end[(0, t - 2)])
+            g.remote_dma_fused([RemoteDMATransfer(dst_ids=[dst(topo, c)], dma_engine_mask=ones[n],
+                                                  remote_sem=sem["fr%d" % s]) for n, c in enumerate(peers)],
+                               local_sem=sem.lc)
+        g.wait_ge(sem.q, t + 1)
+        if t >= 2:
+            g.wait_ge(sem["fr%d" % s], len(peers))
+        to = peers + [me["out"][t]]
+        for buf, codes in ((grp[s], True), (pln[s], False)):
+            g.remote_dma_fused([transfer(topo, buf, own, codes, to, km, sem["aa%d" % t])],
+                               local_sem=sem["la%d" % t])
+    for t in range(KT):
+        g.wait_ge(sem.mm, step_end[(0, t + 2) if t < 2 else (1, t - 2)])
+        if t < 2:
+            g.wait_ge(sem["la%d" % (t + 2)], 2 * kn)
+        rid, pid, _ = topo.addr(me["in"][t])
+        g.remote_sem_update(sem["ce%d" % t], sem.lc, pid, rid, ones[0])
+    g.wait_ge(sem.lc, 2 * len(peers) + KT)
+
+    stores = []
+    free = [None] * S
+    nxt = nv = na = 0
+    bank_done = {}
+    for p in range(2):
+        js = [list(T.cores).index(c) for c in (me if p == 0 else far)["ranks"]]
+        for pair in PAIRS:
+            for col, j in enumerate(js):
+                if nxt + len(pair) > S:
+                    nxt = 0
+                units = list(range(nxt, nxt + len(pair)))
+                nxt = (nxt + len(pair)) % S
+                copies = []
+                for u, i in zip(units, pair):
+                    eng = "v" if i % 2 == 0 else "s"
+                    if eng == "v":
+                        nv += 1
+                    else:
+                        na += 1
+                    copies.append((eng, i, u))
+                    bank_done[(p, i)] = (nv, na)
+                stores.append({"p": p, "j": j, "col": col, "pair": pair, "units": units, "copies": copies,
+                               "after": sorted(set(free[u] for u in units if free[u] is not None)),
+                               "nv": nv, "na": na})
+                for u in units:
+                    free[u] = len(stores) - 1
+
+    seen, order, bank = set(), [], {}
+    for k, (p, t, i) in enumerate(steps):
+        s = k % R
+        b = t % 2
+        if (p, t) not in seen:
+            seen.add((p, t))
+            if p == 0:
+                g.tensor.wait_ge(sem.q, t + 1)
+                g.tensor.wait_ge(sem["aa%d" % t], len(peers) * 2 * kn)
+            else:
+                g.tensor.wait_ge(sem["ab%d" % t], 2 * DE)
+        if (p, i) not in bank:
+            bank[(p, i)] = len(order) % 8
+            if len(order) >= 8:
+                v, a = bank_done[order[len(order) - 8]]
+                if v:
+                    g.tensor.wait_ge(sem.evv, v)
+                if a:
+                    g.tensor.wait_ge(sem.evs, a)
+            order.append((p, i))
+        g.tensor.wait_ge(sem["wl%d" % s], 32 * (k // R + 1))
+        o = 512 * bank[(p, i)]
+        g.tensor.matmul_mx(T.ps[:, o:o + GW], T.wq[:, 128 * s:128 * s + 128], T.wp[:, 128 * s:128 * s + 128],
+                           grp[b][:], pln[b][:], t == 0, t == KT - 1).then_inc(sem.mm, 1)
+
+    for n, st in enumerate(stores):
+        engs = sorted(set(e for e, i, u in st["copies"]))
+        for e in engs:
+            for m in st["after"]:
+                (g.vector if e == "v" else g.scalar).wait_ge(sem["ys%d" % m], 16)
+        for e, i, u in st["copies"]:
+            o = 512 * bank[(st["p"], i)] + 128 * st["col"]
+            if e == "v":
+                g.vector.wait_ge(sem.mm, last[(st["p"], i)])
+                g.vector.tensor_copy(T.yst[:, 128 * u:128 * u + 128], T.ps[:, o:o + 128]).then_inc(sem.evv, 1)
+            else:
+                g.scalar.wait_ge(sem.mm, last[(st["p"], i)])
+                g.scalar.activation(T.yst[:, 128 * u:128 * u + 128], T.ps[:, o:o + 128],
+                                    ActivationFunctionType.Copy).then_inc(sem.evs, 1)
+        if "v" in engs:
+            g.scalar.wait_ge(sem.evv, st["nv"])
+        if "s" in engs:
+            g.scalar.wait_ge(sem.evs, st["na"])
+        o = 128 * (WT * st["j"] + st["pair"][0])
+        u = 128 * st["units"][0]
+        w = 128 * len(st["pair"])
+        g.scalar.dma_start(T.y[:, o:o + w], T.yst[:, u:u + w]).then_inc(sem["ys%d" % n], 16)
+    for n in sorted(set(free)):
+        g.scalar.wait_ge(sem["ys%d" % n], 16)
+
+
+def helper_program(g, core, T, topo, me, far):
+    grp, pln, sem = [T.g0, T.g1], [T.p0, T.p1], T.sem
+    sent = 0
+    for t in range(KT):
+        s = t % 2
+        both = ((grp[s], True), (pln[s], False))
+        if me["out"][t] == core:
+            to = far["in"][t]
+            kn = pick(topo.mask(me["ranks"][0], core), KE, 2)[1]
+            cm, cn = pick(topo.mask(core, to), CE)
+            g.wait_ge(sem["aa%d" % t], GR * 2 * kn)
+            for buf, codes in both:
+                g.remote_dma_fused([transfer(topo, buf, (0, GW), codes, [to], cm, sem["ae%d" % t])], local_sem=sem.lx)
+            sent += 2 * cn
+        if me["in"][t] == core:
+            cn = pick(topo.mask(far["out"][t], core), CE)[1]
+            dm, dn = pick(topo.mask(core, me["ranks"][0]), DE)
+            g.wait_ge(sem["ae%d" % t], 2 * cn)
+            g.wait_ge(sem["ce%d" % t], GR)
+            for buf, codes in both:
+                g.remote_dma_fused([transfer(topo, buf, (0, GW), codes, me["ranks"], dm, sem["ab%d" % t])],
+                                   local_sem=sem.lx)
+            sent += 2 * dn
+    if sent:
+        g.wait_ge(sem.lx, sent)

@@ -7,9 +7,10 @@ R = 4
 S = 4
 GR = 3
 GW = GR * 128
-PAIRS = [(0, 1), (2, 3), (4,)]
+HW = GW // 2
+PAIRS = [(0,), (1,), (2,), (3,), (4,)]
 NST = 2 * GR * len(PAIRS)
-KE = 8
+KE = (8, 16, 16, 16)
 CE = 8
 DE = 16
 
@@ -27,7 +28,7 @@ SCRATCH = {
 SEMAPHORES = (["xl", "q", "mm", "evv", "evs", "lc", "lx"]
               + ["wl%d" % s for s in range(R)]
               + ["ys%d" % n for n in range(NST)]
-              + ["%s%d" % (a, t) for a in ("la", "aa", "ae", "ab", "ce") for t in range(KT)]
+              + ["%s%d" % (a, t) for a in ("la", "aa", "ad", "ae", "ab", "ce") for t in range(KT)]
               + ["fr0", "fr1"])
 
 
@@ -35,8 +36,9 @@ def engines(mask):
     return [1 << b for b in range(mask.bit_length()) if (mask >> b) & 1]
 
 
-def pick(mask, n, step=1):
-    e = engines(mask)[::step][:n]
+def spread(mask, n):
+    e = engines(mask)
+    e = e[::max(1, len(e) // n)][:n]
     return sum(e), len(e)
 
 
@@ -56,18 +58,26 @@ def plan(T, topo):
         o["mate"] = topo.chip(far[0])
         dies = sorted(set(topo.die(c) for c in helpers), reverse=True)
         a, b = [[c for c in helpers if topo.die(c) == d and topo.may_write(c, far[0])] for d in dies]
-        e, f = [[c for c in helpers if topo.die(c) == d and not topo.may_write(c, far[0])] for d in dies]
+        stay = [c for c in helpers if not topo.may_write(c, far[0])]
         o["out"] = [a[0], b[0], b[-1], a[-1]]
-        o["in"] = [e[0], f[0], f[0], e[0]]
+        o["in"] = [stay, b, stay, b]
     return out
 
 
-def transfer(topo, buf, cols, codes, to, mask, rsem):
-    v = buf[:, cols[0]:cols[1]]
-    if codes:
-        v = v.bitcast(dt.uint8)
+def view(buf, a, n, codes):
+    v = buf[:, a:a + n]
+    return v.bitcast(dt.uint8) if codes else v
+
+
+def transfer(topo, src, dsts, to, mask, rsem):
     return RemoteDMATransfer(dst_ids=[dst(topo, c) for c in to], dma_engine_mask=mask,
-                             remote_sem=rsem, srcs=[v], dsts=[v] * len(to))
+                             remote_sem=rsem, srcs=[src], dsts=dsts)
+
+
+def signal(g, topo, to, mask, rsem, lsem):
+    e = engines(mask)
+    g.remote_dma_fused([RemoteDMATransfer(dst_ids=[dst(topo, c)], dma_engine_mask=e[n], remote_sem=rsem)
+                        for n, c in enumerate(to)], local_sem=lsem)
 
 
 def rank_program(g, core, T, topo):
@@ -80,8 +90,8 @@ def rank_program(g, core, T, topo):
     grp, pln, sem = [T.g0, T.g1], [T.p0, T.p1], T.sem
     mine = me["ranks"].index(core)
     peers = [c for c in me["ranks"] if c != core]
-    own = (128 * mine, 128 * mine + 128)
-    km, kn = pick(topo.mask(core, peers[0]), KE, 2)
+    own = 128 * mine
+    near = [spread(topo.mask(core, peers[0]), n) for n in KE]
 
     steps = [(p, t, i) for p in range(2) for t in range(KT) for i in range(WT)]
     step_end = {}
@@ -96,9 +106,10 @@ def rank_program(g, core, T, topo):
         n = KT * i + t
         if k >= R:
             g.sync.wait_ge(sem.mm, k - R + 1)
-        w = T.wq[:, 128 * s:128 * s + 128].bitcast(dt.uint8)
-        g.sync.dma_start(w, T.wc[:, 512 * n:512 * n + 512]).then_inc(sem["wl%d" % s], 16)
-        g.sync.dma_start(T.wp[:, 128 * s:128 * s + 128], T.ws[:, 128 * n:128 * n + 128]).then_inc(sem["wl%d" % s], 16)
+        g.sync.dma_start(view(T.wq, 128 * s, 128, True),
+                         T.wc[:, 512 * n:512 * n + 512]).then_inc(sem["wl%d" % s], 16)
+        g.sync.dma_start(view(T.wp, 128 * s, 128, False),
+                         T.ws[:, 128 * n:128 * n + 128]).then_inc(sem["wl%d" % s], 16)
 
     for t in range(1, KT):
         g.scalar.wait_ge(sem.q, t)
@@ -108,32 +119,29 @@ def rank_program(g, core, T, topo):
         s = t % 2
         if t >= 2:
             g.vector.wait_ge(sem.mm, step_end[(0, t - 2)])
-            g.vector.wait_ge(sem["la%d" % (t - 2)], 2 * kn)
+            g.vector.wait_ge(sem["la%d" % (t - 2)], 4 * near[t - 2][1])
         g.vector.wait_ge(sem.xl, 16 * (t + 1))
-        g.vector.quantize_mx(grp[s][:, own[0]:own[1]], pln[s][:, own[0]:own[1]], T.xb[:]).then_inc(sem.q, 1)
+        g.vector.quantize_mx(grp[s][:, own:own + 128], pln[s][:, own:own + 128], T.xb[:]).then_inc(sem.q, 1)
 
-    ones = engines(km)
     for t in range(KT):
         s = t % 2
+        km = near[t][0]
         if t >= 2:
             g.wait_ge(sem.mm, step_end[(0, t - 2)])
-            g.remote_dma_fused([RemoteDMATransfer(dst_ids=[dst(topo, c)], dma_engine_mask=ones[n],
-                                                  remote_sem=sem["fr%d" % s]) for n, c in enumerate(peers)],
-                               local_sem=sem.lc)
+            signal(g, topo, peers, km, sem["fr%d" % s], sem.lc)
         g.wait_ge(sem.q, t + 1)
         if t >= 2:
             g.wait_ge(sem["fr%d" % s], len(peers))
-        to = peers + [me["out"][t]]
-        for buf, codes in ((grp[s], True), (pln[s], False)):
-            g.remote_dma_fused([transfer(topo, buf, own, codes, to, km, sem["aa%d" % t])],
-                               local_sem=sem["la%d" % t])
+        for to, rsem in ((peers, sem["aa%d" % t]), ([me["out"][t]], sem["ad%d" % t])):
+            for buf, codes in ((grp[s], True), (pln[s], False)):
+                v = view(buf, own, 128, codes)
+                g.remote_dma_fused([transfer(topo, v, [v] * len(to), to, km, rsem)], local_sem=sem["la%d" % t])
     for t in range(KT):
         g.wait_ge(sem.mm, step_end[(0, t + 2) if t < 2 else (1, t - 2)])
         if t < 2:
-            g.wait_ge(sem["la%d" % (t + 2)], 2 * kn)
-        rid, pid, _ = topo.addr(me["in"][t])
-        g.remote_sem_update(sem["ce%d" % t], sem.lc, pid, rid, ones[0])
-    g.wait_ge(sem.lc, 2 * len(peers) + KT)
+            g.wait_ge(sem["la%d" % (t + 2)], 4 * near[t + 2][1])
+        signal(g, topo, me["in"][t], near[0][0], sem["ce%d" % t], sem.lc)
+    g.wait_ge(sem.lc, 2 * len(peers) + sum(len(c) for c in me["in"]))
 
     stores = []
     free = [None] * S
@@ -170,9 +178,9 @@ def rank_program(g, core, T, topo):
             seen.add((p, t))
             if p == 0:
                 g.tensor.wait_ge(sem.q, t + 1)
-                g.tensor.wait_ge(sem["aa%d" % t], len(peers) * 2 * kn)
+                g.tensor.wait_ge(sem["aa%d" % t], len(peers) * 2 * near[t][1])
             else:
-                g.tensor.wait_ge(sem["ab%d" % t], 2 * DE)
+                g.tensor.wait_ge(sem["ab%d" % t], 2 * 2 * DE)
         if (p, i) not in bank:
             bank[(p, i)] = len(order) % 8
             if len(order) >= 8:
@@ -216,25 +224,30 @@ def rank_program(g, core, T, topo):
 def helper_program(g, core, T, topo, me, far):
     grp, pln, sem = [T.g0, T.g1], [T.p0, T.p1], T.sem
     sent = 0
-    for t in range(KT):
+    for role, t in (("out", 0), ("out", 1), ("out", 2), ("in", 0), ("out", 3), ("in", 1), ("in", 2), ("in", 3)):
         s = t % 2
-        both = ((grp[s], True), (pln[s], False))
-        if me["out"][t] == core:
+        keep = 256 * (t // 2)
+        if role == "out" and me["out"][t] == core:
+            kn = spread(topo.mask(me["ranks"][0], core), KE[t])[1]
+            g.wait_ge(sem["ad%d" % t], GR * 2 * kn)
             to = far["in"][t]
-            kn = pick(topo.mask(me["ranks"][0], core), KE, 2)[1]
-            cm, cn = pick(topo.mask(core, to), CE)
-            g.wait_ge(sem["aa%d" % t], GR * 2 * kn)
-            for buf, codes in both:
-                g.remote_dma_fused([transfer(topo, buf, (0, GW), codes, [to], cm, sem["ae%d" % t])], local_sem=sem.lx)
-            sent += 2 * cn
-        if me["in"][t] == core:
-            cn = pick(topo.mask(far["out"][t], core), CE)[1]
-            dm, dn = pick(topo.mask(core, me["ranks"][0]), DE)
+            e = spread(topo.mask(core, to[0]), CE)[0]
+            e = engines(e)
+            for src, kept, codes in ((grp[s], T.wq, True), (pln[s], T.wp, False)):
+                g.remote_dma_fused([transfer(topo, view(src, HW * h, HW, codes), [view(kept, keep, HW, codes)], [c],
+                                             sum(e[h::2]), sem["ae%d" % t]) for h, c in enumerate(to)],
+                                   local_sem=sem.lx)
+            sent += 2 * len(e)
+        if role == "in" and core in me["in"][t]:
+            h = me["in"][t].index(core)
+            cn = spread(topo.mask(far["out"][t], core), CE)[1] // 2
+            dm, dn = spread(topo.mask(core, me["ranks"][0]), DE)
             g.wait_ge(sem["ae%d" % t], 2 * cn)
             g.wait_ge(sem["ce%d" % t], GR)
-            for buf, codes in both:
-                g.remote_dma_fused([transfer(topo, buf, (0, GW), codes, me["ranks"], dm, sem["ab%d" % t])],
-                                   local_sem=sem.lx)
+            for kept, out, codes in ((T.wq, grp[s], True), (T.wp, pln[s], False)):
+                d = view(out, HW * h, HW, codes)
+                g.remote_dma_fused([transfer(topo, view(kept, keep, HW, codes), [d] * GR, me["ranks"], dm,
+                                             sem["ab%d" % t])], local_sem=sem.lx)
             sent += 2 * dn
     if sent:
         g.wait_ge(sem.lx, sent)

@@ -8,11 +8,21 @@ S = 4
 GR = 3
 GW = GR * 128
 HW = GW // 2
-PAIRS = [(0,), (1,), (2,), (3,), (4,)]
-NST = 2 * GR * len(PAIRS)
+NIN = 3
 KE = (8, 16, 16, 16)
 CE = 8
 DE = 16
+NB = GR * WT
+WHOLE, FIRST, SECOND = (0, 128), (0, 64), (64, 64)
+
+
+def store_order():
+    a = [(n, WHOLE) for n in range(NB)]
+    b = list(a)
+    b[S] = (S, FIRST)
+    b.insert(2 * S + 1, (S, SECOND))
+    return a, b
+
 
 SCRATCH = {
     "xb": ("sbuf", [128, 512], "bfloat16"),
@@ -22,13 +32,16 @@ SCRATCH = {
     "p1": ("sbuf", [128, GW], "uint8"),
     "wq": ("sbuf", [128, R * 128], "float8_e4m3fn_x4"),
     "wp": ("sbuf", [128, R * 128], "uint8"),
-    "yst": ("sbuf", [128, S * 128], "float32"),
+    "yst": ("sbuf", [128, S * 128 + 64], "float32"),
     "ps": ("psum", [128, 8 * 512], "float32"),
 }
+for _t in range(KT):
+    SCRATCH["kq%d" % _t] = ("dram", [128, HW], "float8_e4m3fn_x4")
+    SCRATCH["kp%d" % _t] = ("dram", [128, GW], "uint8")
 SEMAPHORES = (["xl", "q", "mm", "evv", "evs", "lc", "lx"]
               + ["wl%d" % s for s in range(R)]
-              + ["ys%d" % n for n in range(NST)]
-              + ["%s%d" % (a, t) for a in ("la", "aa", "ad", "ae", "ab", "ce") for t in range(KT)]
+              + ["ys%d" % n for n in range(S + 1)]
+              + ["%s%d" % (a, t) for a in ("la", "lo", "aa", "ad", "ae", "ab", "ce") for t in range(KT)]
               + ["fr0", "fr1"])
 
 
@@ -58,9 +71,8 @@ def plan(T, topo):
         o["mate"] = topo.chip(far[0])
         dies = sorted(set(topo.die(c) for c in helpers), reverse=True)
         a, b = [[c for c in helpers if topo.die(c) == d and topo.may_write(c, far[0])] for d in dies]
-        stay = [c for c in helpers if not topo.may_write(c, far[0])]
         o["out"] = [a[0], b[0], b[-1], a[-1]]
-        o["in"] = [stay, b, stay, b]
+        o["in"] = sorted(set(a + b))[:NIN]
     return out
 
 
@@ -94,11 +106,11 @@ def rank_program(g, core, T, topo):
     near = [spread(topo.mask(core, peers[0]), n) for n in KE]
 
     steps = [(p, t, i) for p in range(2) for t in range(KT) for i in range(WT)]
-    step_end = {}
-    last = {}
+    first, last, step_end = {}, {}, {}
     for k, (p, t, i) in enumerate(steps):
+        first.setdefault((p, i), k)
+        last[(p, i)] = k
         step_end[(p, t)] = k + 1
-        last[(p, i)] = k + 1
 
     g.sync.dma_start(T.xb[:], T.x[:, 0:512]).then_inc(sem.xl, 16)
     for k, (p, t, i) in enumerate(steps):
@@ -115,139 +127,127 @@ def rank_program(g, core, T, topo):
         g.scalar.wait_ge(sem.q, t)
         g.scalar.dma_start(T.xb[:], T.x[:, 512 * t:512 * t + 512]).then_inc(sem.xl, 16)
 
+    def left(q, t):
+        q.wait_ge(sem["la%d" % t], 2 * near[t][1])
+        q.wait_ge(sem["lo%d" % t], 2 * near[t][1])
+
     for t in range(KT):
         s = t % 2
         if t >= 2:
             g.vector.wait_ge(sem.mm, step_end[(0, t - 2)])
-            g.vector.wait_ge(sem["la%d" % (t - 2)], 4 * near[t - 2][1])
+            left(g.vector, t - 2)
         g.vector.wait_ge(sem.xl, 16 * (t + 1))
         g.vector.quantize_mx(grp[s][:, own:own + 128], pln[s][:, own:own + 128], T.xb[:]).then_inc(sem.q, 1)
 
+    def send(t, to, rsem, lsem):
+        for buf, codes in ((grp[t % 2], True), (pln[t % 2], False)):
+            v = view(buf, own, 128, codes)
+            g.remote_dma_fused([transfer(topo, v, [v] * len(to), to, near[t][0], rsem)], local_sem=lsem)
+
     for t in range(KT):
         s = t % 2
-        km = near[t][0]
         if t >= 2:
             g.wait_ge(sem.mm, step_end[(0, t - 2)])
-            signal(g, topo, peers, km, sem["fr%d" % s], sem.lc)
+            signal(g, topo, peers, near[t][0], sem["fr%d" % s], sem.lc)
         g.wait_ge(sem.q, t + 1)
+        collector = ([me["out"][t]], sem["ad%d" % t], sem["lo%d" % t])
         if t >= 2:
+            send(t, *collector)
             g.wait_ge(sem["fr%d" % s], len(peers))
-        for to, rsem in ((peers, sem["aa%d" % t]), ([me["out"][t]], sem["ad%d" % t])):
-            for buf, codes in ((grp[s], True), (pln[s], False)):
-                v = view(buf, own, 128, codes)
-                g.remote_dma_fused([transfer(topo, v, [v] * len(to), to, km, rsem)], local_sem=sem["la%d" % t])
+        send(t, peers, sem["aa%d" % t], sem["la%d" % t])
+        if t < 2:
+            send(t, *collector)
     for t in range(KT):
         g.wait_ge(sem.mm, step_end[(0, t + 2) if t < 2 else (1, t - 2)])
         if t < 2:
-            g.wait_ge(sem["la%d" % (t + 2)], 4 * near[t + 2][1])
-        signal(g, topo, me["in"][t], near[0][0], sem["ce%d" % t], sem.lc)
-    g.wait_ge(sem.lc, 2 * len(peers) + sum(len(c) for c in me["in"]))
+            left(g, t + 2)
+        signal(g, topo, me["in"], near[0][0], sem["ce%d" % t], sem.lc)
+    g.wait_ge(sem.lc, 2 * len(peers) + KT * NIN)
 
     stores = []
-    free = [None] * S
+    count = [0] * (S + 1)
     nxt = nv = na = 0
     bank_done = {}
     for p in range(2):
-        js = [list(T.cores).index(c) for c in (me if p == 0 else far)["ranks"]]
-        for pair in PAIRS:
-            for col, j in enumerate(js):
-                if nxt + len(pair) > S:
-                    nxt = 0
-                units = list(range(nxt, nxt + len(pair)))
-                nxt = (nxt + len(pair)) % S
-                copies = []
-                for u, i in zip(units, pair):
-                    eng = "v" if i % 2 == 0 else "s"
-                    if eng == "v":
-                        nv += 1
-                    else:
-                        na += 1
-                    copies.append((eng, i, u))
-                    bank_done[(p, i)] = (nv, na)
-                stores.append({"p": p, "j": j, "col": col, "pair": pair, "units": units, "copies": copies,
-                               "after": sorted(set(free[u] for u in units if free[u] is not None)),
-                               "nv": nv, "na": na})
-                for u in units:
-                    free[u] = len(stores) - 1
+        for n, (c0, cw) in store_order()[p]:
+            i, col = divmod(n, GR)
+            vec = (i + p) % 2 == 0
+            nv, na = nv + vec, na + (not vec)
+            if (c0, cw) == WHOLE:
+                u, nxt = nxt, (nxt + 1) % S
+            else:
+                u = S
+            j = T.rank_of((me if p == 0 else far)["ranks"][col])
+            stores.append((p, i, col, j, c0, cw, u, count[u], vec, nv, na))
+            count[u] += 1
+            bank_done[(p, i)] = (vec, nv if vec else na)
 
-    seen, order, bank = set(), [], {}
+    order = sorted(first, key=first.get)
+    bank = {a: n % 8 for n, a in enumerate(order)}
     for k, (p, t, i) in enumerate(steps):
         s = k % R
         b = t % 2
-        if (p, t) not in seen:
-            seen.add((p, t))
+        if i == 0:
             if p == 0:
                 g.tensor.wait_ge(sem.q, t + 1)
                 g.tensor.wait_ge(sem["aa%d" % t], len(peers) * 2 * near[t][1])
             else:
-                g.tensor.wait_ge(sem["ab%d" % t], 2 * 2 * DE)
-        if (p, i) not in bank:
-            bank[(p, i)] = len(order) % 8
-            if len(order) >= 8:
-                v, a = bank_done[order[len(order) - 8]]
-                if v:
-                    g.tensor.wait_ge(sem.evv, v)
-                if a:
-                    g.tensor.wait_ge(sem.evs, a)
-            order.append((p, i))
+                g.tensor.wait_ge(sem["ab%d" % t], NIN * DE)
+        n = order.index((p, i))
+        if t == 0 and n >= 8:
+            vec, c = bank_done[order[n - 8]]
+            g.tensor.wait_ge(sem.evv if vec else sem.evs, c)
         g.tensor.wait_ge(sem["wl%d" % s], 32 * (k // R + 1))
         o = 512 * bank[(p, i)]
         g.tensor.matmul_mx(T.ps[:, o:o + GW], T.wq[:, 128 * s:128 * s + 128], T.wp[:, 128 * s:128 * s + 128],
                            grp[b][:], pln[b][:], t == 0, t == KT - 1).then_inc(sem.mm, 1)
 
-    for n, st in enumerate(stores):
-        engs = sorted(set(e for e, i, u in st["copies"]))
-        for e in engs:
-            for m in st["after"]:
-                (g.vector if e == "v" else g.scalar).wait_ge(sem["ys%d" % m], 16)
-        for e, i, u in st["copies"]:
-            o = 512 * bank[(st["p"], i)] + 128 * st["col"]
-            if e == "v":
-                g.vector.wait_ge(sem.mm, last[(st["p"], i)])
-                g.vector.tensor_copy(T.yst[:, 128 * u:128 * u + 128], T.ps[:, o:o + 128]).then_inc(sem.evv, 1)
-            else:
-                g.scalar.wait_ge(sem.mm, last[(st["p"], i)])
-                g.scalar.activation(T.yst[:, 128 * u:128 * u + 128], T.ps[:, o:o + 128],
-                                    ActivationFunctionType.Copy).then_inc(sem.evs, 1)
-        if "v" in engs:
-            g.scalar.wait_ge(sem.evv, st["nv"])
-        if "s" in engs:
-            g.scalar.wait_ge(sem.evs, st["na"])
-        o = 128 * (WT * st["j"] + st["pair"][0])
-        u = 128 * st["units"][0]
-        w = 128 * len(st["pair"])
-        g.scalar.dma_start(T.y[:, o:o + w], T.yst[:, u:u + w]).then_inc(sem["ys%d" % n], 16)
-    for n in sorted(set(free)):
-        g.scalar.wait_ge(sem["ys%d" % n], 16)
+    for p, i, col, j, c0, cw, u, before, vec, nv, na in stores:
+        q = g.vector if vec else g.scalar
+        if before:
+            q.wait_ge(sem["ys%d" % u], 16 * before)
+        q.wait_ge(sem.mm, last[(p, i)] + 1)
+        o = 512 * bank[(p, i)] + 128 * col + c0
+        unit = T.yst[:, 128 * u:128 * u + cw]
+        if vec:
+            g.vector.tensor_copy(unit, T.ps[:, o:o + cw]).then_inc(sem.evv, 1)
+            g.scalar.wait_ge(sem.evv, nv)
+        else:
+            g.scalar.activation(unit, T.ps[:, o:o + cw], ActivationFunctionType.Copy).then_inc(sem.evs, 1)
+            g.scalar.wait_ge(sem.evs, na)
+        o = 128 * (WT * j + i) + c0
+        g.scalar.dma_start(T.y[:, o:o + cw], unit).then_inc(sem["ys%d" % u], 16)
+    for u in range(S + 1):
+        g.scalar.wait_ge(sem["ys%d" % u], 16 * count[u])
 
 
 def helper_program(g, core, T, topo, me, far):
     grp, pln, sem = [T.g0, T.g1], [T.p0, T.p1], T.sem
     sent = 0
-    for role, t in (("out", 0), ("out", 1), ("out", 2), ("in", 0), ("out", 3), ("in", 1), ("in", 2), ("in", 3)):
+    for role, t in [("out", t) for t in range(KT)] + [("in", t) for t in range(KT)]:
         s = t % 2
-        keep = 256 * (t // 2)
+        kq, kp = T["kq%d" % t], T["kp%d" % t]
         if role == "out" and me["out"][t] == core:
             kn = spread(topo.mask(me["ranks"][0], core), KE[t])[1]
             g.wait_ge(sem["ad%d" % t], GR * 2 * kn)
-            to = far["in"][t]
-            e = spread(topo.mask(core, to[0]), CE)[0]
-            e = engines(e)
-            for src, kept, codes in ((grp[s], T.wq, True), (pln[s], T.wp, False)):
-                g.remote_dma_fused([transfer(topo, view(src, HW * h, HW, codes), [view(kept, keep, HW, codes)], [c],
-                                             sum(e[h::2]), sem["ae%d" % t]) for h, c in enumerate(to)],
-                                   local_sem=sem.lx)
-            sent += 2 * len(e)
-        if role == "in" and core in me["in"][t]:
-            h = me["in"][t].index(core)
+            to = far["in"]
+            e = engines(spread(topo.mask(core, to[0]), CE)[0])
+            g.remote_dma_fused([transfer(topo, view(grp[s], HW * h, HW, True), [view(kq, 0, HW, True)], [to[h]],
+                                         sum(e[h::2]), sem["ae%d" % t]) for h in range(2)], local_sem=sem.lx)
+            g.remote_dma_fused([transfer(topo, view(pln[s], 0, GW, False), [view(kp, 0, GW, False)], [to[2]],
+                                         sum(e[0::2]), sem["ae%d" % t])], local_sem=sem.lx)
+            sent += len(e) + len(e[0::2])
+        if role == "in" and core in me["in"]:
+            h = me["in"].index(core)
             cn = spread(topo.mask(far["out"][t], core), CE)[1] // 2
             dm, dn = spread(topo.mask(core, me["ranks"][0]), DE)
-            g.wait_ge(sem["ae%d" % t], 2 * cn)
+            g.wait_ge(sem["ae%d" % t], cn)
             g.wait_ge(sem["ce%d" % t], GR)
-            for kept, out, codes in ((T.wq, grp[s], True), (T.wp, pln[s], False)):
-                d = view(out, HW * h, HW, codes)
-                g.remote_dma_fused([transfer(topo, view(kept, keep, HW, codes), [d] * GR, me["ranks"], dm,
-                                             sem["ab%d" % t])], local_sem=sem.lx)
-            sent += 2 * dn
+            if h < 2:
+                a, d = view(kq, 0, HW, True), view(grp[s], HW * h, HW, True)
+            else:
+                a, d = view(kp, 0, GW, False), view(pln[s], 0, GW, False)
+            g.remote_dma_fused([transfer(topo, a, [d] * GR, me["ranks"], dm, sem["ab%d" % t])], local_sem=sem.lx)
+            sent += dn
     if sent:
         g.wait_ge(sem.lx, sent)

@@ -1,5 +1,5 @@
 from concourse.bass import DstId, RemoteDMATransfer
-from concourse.mybir import dt, ActivationFunctionType
+from concourse.mybir import dt
 
 KT, WT = 4, 5
 NCORES = 16
@@ -9,11 +9,21 @@ GR = 3
 GW = GR * 128
 HW = GW // 2
 NIN = 3
-KE = (8, 16, 16, 16)
+KE = 16
 CE = 8
 DE = 16
 NB = GR * WT
+LAST = KT - 1
 WHOLE, FIRST, SECOND = (0, 128), (0, 64), (64, 64)
+
+
+def product_order():
+    steps = [(p, t, i) for p in range(2) for t in range(KT) for i in range(WT)][:-2 * WT]
+    a, b = [(1, LAST - 1, i) for i in range(WT)], [(1, LAST, i) for i in range(WT)]
+    steps += a[:2] + b[:2]
+    for i in range(2, WT):
+        steps += [a[i], b[i]]
+    return steps
 
 
 def store_order():
@@ -34,11 +44,14 @@ SCRATCH = {
     "wp": ("sbuf", [128, R * 128], "uint8"),
     "yst": ("sbuf", [128, S * 128 + 64], "float32"),
     "ps": ("psum", [128, 8 * 512], "float32"),
+    "hq0": ("dram", [128, HW], "float8_e4m3fn_x4"),
+    "hq1": ("dram", [128, HW], "float8_e4m3fn_x4"),
+    "hp": ("dram", [128, GW], "uint8"),
 }
 for _t in range(KT):
     SCRATCH["kq%d" % _t] = ("dram", [128, HW], "float8_e4m3fn_x4")
     SCRATCH["kp%d" % _t] = ("dram", [128, GW], "uint8")
-SEMAPHORES = (["xl", "q", "mm", "evv", "evs", "lc", "lx"]
+SEMAPHORES = (["xl", "q", "mm", "ev", "lc", "lx", "gl"]
               + ["wl%d" % s for s in range(R)]
               + ["ys%d" % n for n in range(S + 1)]
               + ["%s%d" % (a, t) for a in ("la", "lo", "aa", "ad", "ae", "ab", "ce") for t in range(KT)]
@@ -103,19 +116,27 @@ def rank_program(g, core, T, topo):
     mine = me["ranks"].index(core)
     peers = [c for c in me["ranks"] if c != core]
     own = 128 * mine
-    near = [spread(topo.mask(core, peers[0]), n) for n in KE]
+    near, nn = spread(topo.mask(core, peers[0]), KE)
 
-    steps = [(p, t, i) for p in range(2) for t in range(KT) for i in range(WT)]
-    first, last, step_end = {}, {}, {}
+    steps = product_order()
+    first, last, begin, end = {}, {}, {}, {}
     for k, (p, t, i) in enumerate(steps):
         first.setdefault((p, i), k)
         last[(p, i)] = k
-        step_end[(p, t)] = k + 1
+        begin.setdefault((p, t), k)
+        end[(p, t)] = k + 1
 
     g.sync.dma_start(T.xb[:], T.x[:, 0:512]).then_inc(sem.xl, 16)
     for k, (p, t, i) in enumerate(steps):
         s = k % R
         n = KT * i + t
+        if k - R + 1 == end[(1, LAST - 2)]:
+            b = LAST % 2
+            g.sync.wait_ge(sem.mm, end[(1, LAST - 2)])
+            g.sync.wait_ge(sem["ab%d" % LAST], NIN * DE)
+            for h, part in enumerate((T.hq0, T.hq1)):
+                g.sync.dma_start(view(grp[b], HW * h, HW, True), view(part, 0, HW, True)).then_inc(sem.gl, 16)
+            g.sync.dma_start(view(pln[b], 0, GW, False), view(T.hp, 0, GW, False)).then_inc(sem.gl, 16)
         if k >= R:
             g.sync.wait_ge(sem.mm, k - R + 1)
         g.sync.dma_start(view(T.wq, 128 * s, 128, True),
@@ -128,13 +149,13 @@ def rank_program(g, core, T, topo):
         g.scalar.dma_start(T.xb[:], T.x[:, 512 * t:512 * t + 512]).then_inc(sem.xl, 16)
 
     def left(q, t):
-        q.wait_ge(sem["la%d" % t], 2 * near[t][1])
-        q.wait_ge(sem["lo%d" % t], 2 * near[t][1])
+        q.wait_ge(sem["la%d" % t], 2 * nn)
+        q.wait_ge(sem["lo%d" % t], 2 * nn)
 
     for t in range(KT):
         s = t % 2
         if t >= 2:
-            g.vector.wait_ge(sem.mm, step_end[(0, t - 2)])
+            g.vector.wait_ge(sem.mm, end[(0, t - 2)])
             left(g.vector, t - 2)
         g.vector.wait_ge(sem.xl, 16 * (t + 1))
         g.vector.quantize_mx(grp[s][:, own:own + 128], pln[s][:, own:own + 128], T.xb[:]).then_inc(sem.q, 1)
@@ -142,13 +163,13 @@ def rank_program(g, core, T, topo):
     def send(t, to, rsem, lsem):
         for buf, codes in ((grp[t % 2], True), (pln[t % 2], False)):
             v = view(buf, own, 128, codes)
-            g.remote_dma_fused([transfer(topo, v, [v] * len(to), to, near[t][0], rsem)], local_sem=lsem)
+            g.remote_dma_fused([transfer(topo, v, [v] * len(to), to, near, rsem)], local_sem=lsem)
 
     for t in range(KT):
         s = t % 2
         if t >= 2:
-            g.wait_ge(sem.mm, step_end[(0, t - 2)])
-            signal(g, topo, peers, near[t][0], sem["fr%d" % s], sem.lc)
+            g.wait_ge(sem.mm, end[(0, t - 2)])
+            signal(g, topo, peers, near, sem["fr%d" % s], sem.lc)
         g.wait_ge(sem.q, t + 1)
         collector = ([me["out"][t]], sem["ad%d" % t], sem["lo%d" % t])
         if t >= 2:
@@ -158,63 +179,60 @@ def rank_program(g, core, T, topo):
         if t < 2:
             send(t, *collector)
     for t in range(KT):
-        g.wait_ge(sem.mm, step_end[(0, t + 2) if t < 2 else (1, t - 2)])
         if t < 2:
+            g.wait_ge(sem.mm, end[(0, t + 2)])
             left(g, t + 2)
-        signal(g, topo, me["in"], near[0][0], sem["ce%d" % t], sem.lc)
-    g.wait_ge(sem.lc, 2 * len(peers) + KT * NIN)
+        elif t < LAST:
+            g.wait_ge(sem.mm, end[(1, t - 2)])
+        if t < LAST:
+            signal(g, topo, me["in"], near, sem["ce%d" % t], sem.lc)
+    g.wait_ge(sem.lc, 2 * len(peers) + LAST * NIN)
 
     stores = []
     count = [0] * (S + 1)
-    nxt = nv = na = 0
+    nxt = 0
     bank_done = {}
     for p in range(2):
         for n, (c0, cw) in store_order()[p]:
             i, col = divmod(n, GR)
-            vec = (i + p) % 2 == 0
-            nv, na = nv + vec, na + (not vec)
             if (c0, cw) == WHOLE:
                 u, nxt = nxt, (nxt + 1) % S
             else:
                 u = S
             j = T.rank_of((me if p == 0 else far)["ranks"][col])
-            stores.append((p, i, col, j, c0, cw, u, count[u], vec, nv, na))
+            stores.append((p, i, col, j, c0, cw, u, count[u]))
             count[u] += 1
-            bank_done[(p, i)] = (vec, nv if vec else na)
+            bank_done[(p, i)] = len(stores)
 
     order = sorted(first, key=first.get)
     bank = {a: n % 8 for n, a in enumerate(order)}
     for k, (p, t, i) in enumerate(steps):
         s = k % R
         b = t % 2
-        if i == 0:
+        if k == begin[(p, t)]:
             if p == 0:
                 g.tensor.wait_ge(sem.q, t + 1)
-                g.tensor.wait_ge(sem["aa%d" % t], len(peers) * 2 * near[t][1])
-            else:
+                g.tensor.wait_ge(sem["aa%d" % t], len(peers) * 2 * nn)
+            elif t < LAST:
                 g.tensor.wait_ge(sem["ab%d" % t], NIN * DE)
+            else:
+                g.tensor.wait_ge(sem.gl, 16 * 3)
         n = order.index((p, i))
         if t == 0 and n >= 8:
-            vec, c = bank_done[order[n - 8]]
-            g.tensor.wait_ge(sem.evv if vec else sem.evs, c)
+            g.tensor.wait_ge(sem.ev, bank_done[order[n - 8]])
         g.tensor.wait_ge(sem["wl%d" % s], 32 * (k // R + 1))
         o = 512 * bank[(p, i)]
         g.tensor.matmul_mx(T.ps[:, o:o + GW], T.wq[:, 128 * s:128 * s + 128], T.wp[:, 128 * s:128 * s + 128],
                            grp[b][:], pln[b][:], t == 0, t == KT - 1).then_inc(sem.mm, 1)
 
-    for p, i, col, j, c0, cw, u, before, vec, nv, na in stores:
-        q = g.vector if vec else g.scalar
+    for m, (p, i, col, j, c0, cw, u, before) in enumerate(stores):
         if before:
-            q.wait_ge(sem["ys%d" % u], 16 * before)
-        q.wait_ge(sem.mm, last[(p, i)] + 1)
+            g.vector.wait_ge(sem["ys%d" % u], 16 * before)
+        g.vector.wait_ge(sem.mm, last[(p, i)] + 1)
         o = 512 * bank[(p, i)] + 128 * col + c0
         unit = T.yst[:, 128 * u:128 * u + cw]
-        if vec:
-            g.vector.tensor_copy(unit, T.ps[:, o:o + cw]).then_inc(sem.evv, 1)
-            g.scalar.wait_ge(sem.evv, nv)
-        else:
-            g.scalar.activation(unit, T.ps[:, o:o + cw], ActivationFunctionType.Copy).then_inc(sem.evs, 1)
-            g.scalar.wait_ge(sem.evs, na)
+        g.vector.tensor_copy(unit, T.ps[:, o:o + cw]).then_inc(sem.ev, 1)
+        g.scalar.wait_ge(sem.ev, m + 1)
         o = 128 * (WT * j + i) + c0
         g.scalar.dma_start(T.y[:, o:o + cw], unit).then_inc(sem["ys%d" % u], 16)
     for u in range(S + 1):
@@ -224,11 +242,13 @@ def rank_program(g, core, T, topo):
 def helper_program(g, core, T, topo, me, far):
     grp, pln, sem = [T.g0, T.g1], [T.p0, T.p1], T.sem
     sent = 0
-    for role, t in [("out", t) for t in range(KT)] + [("in", t) for t in range(KT)]:
+    ins = list(range(KT))
+    ins[-2:] = [LAST, LAST - 1]
+    for role, t in [("out", t) for t in range(KT)] + [("in", t) for t in ins]:
         s = t % 2
         kq, kp = T["kq%d" % t], T["kp%d" % t]
         if role == "out" and me["out"][t] == core:
-            kn = spread(topo.mask(me["ranks"][0], core), KE[t])[1]
+            kn = spread(topo.mask(me["ranks"][0], core), KE)[1]
             g.wait_ge(sem["ad%d" % t], GR * 2 * kn)
             to = far["in"]
             e = engines(spread(topo.mask(core, to[0]), CE)[0])
@@ -242,11 +262,12 @@ def helper_program(g, core, T, topo, me, far):
             cn = spread(topo.mask(far["out"][t], core), CE)[1] // 2
             dm, dn = spread(topo.mask(core, me["ranks"][0]), DE)
             g.wait_ge(sem["ae%d" % t], cn)
-            g.wait_ge(sem["ce%d" % t], GR)
-            if h < 2:
-                a, d = view(kq, 0, HW, True), view(grp[s], HW * h, HW, True)
+            a = view(kq, 0, HW, True) if h < 2 else view(kp, 0, GW, False)
+            if t == LAST:
+                d = view((T.hq0, T.hq1)[h], 0, HW, True) if h < 2 else view(T.hp, 0, GW, False)
             else:
-                a, d = view(kp, 0, GW, False), view(pln[s], 0, GW, False)
+                g.wait_ge(sem["ce%d" % t], GR)
+                d = view(grp[s], HW * h, HW, True) if h < 2 else view(pln[s], 0, GW, False)
             g.remote_dma_fused([transfer(topo, a, [d] * GR, me["ranks"], dm, sem["ab%d" % t])], local_sem=sem.lx)
             sent += dn
     if sent:

from concourse.bass import DstId, RemoteDMATransfer
from concourse.mybir import dt

KT, WT = 4, 5
NCORES = 16
R = 4
S = 4
GR = 3
GW = GR * 128
HW = GW // 2
NIN = 3
KE = 16
CE = 8
DE = 16
NB = GR * WT
LAST = KT - 1
WHOLE, FIRST, SECOND = (0, 128), (0, 64), (64, 64)


def product_order():
    steps = [(p, t, i) for p in range(2) for t in range(KT) for i in range(WT)][:-2 * WT]
    a, b = [(1, LAST - 1, i) for i in range(WT)], [(1, LAST, i) for i in range(WT)]
    steps += a[:2] + b[:2]
    for i in range(2, WT):
        steps += [a[i], b[i]]
    return steps


def store_order():
    a = [(n, WHOLE) for n in range(NB)]
    b = list(a)
    b[S] = (S, FIRST)
    b.insert(2 * S + 1, (S, SECOND))
    return a, b


SCRATCH = {
    "xb": ("sbuf", [128, 512], "bfloat16"),
    "g0": ("sbuf", [128, GW], "float8_e4m3fn_x4"),
    "g1": ("sbuf", [128, GW], "float8_e4m3fn_x4"),
    "p0": ("sbuf", [128, GW], "uint8"),
    "p1": ("sbuf", [128, GW], "uint8"),
    "wq": ("sbuf", [128, R * 128], "float8_e4m3fn_x4"),
    "wp": ("sbuf", [128, R * 128], "uint8"),
    "yst": ("sbuf", [128, S * 128 + 64], "float32"),
    "ps": ("psum", [128, 8 * 512], "float32"),
    "hq0": ("dram", [128, HW], "float8_e4m3fn_x4"),
    "hq1": ("dram", [128, HW], "float8_e4m3fn_x4"),
    "hp": ("dram", [128, GW], "uint8"),
}
for _t in range(KT):
    SCRATCH["kq%d" % _t] = ("dram", [128, HW], "float8_e4m3fn_x4")
    SCRATCH["kp%d" % _t] = ("dram", [128, GW], "uint8")
SEMAPHORES = (["xl", "q", "mm", "ev", "lc", "lx", "gl"]
              + ["wl%d" % s for s in range(R)]
              + ["ys%d" % n for n in range(S + 1)]
              + ["%s%d" % (a, t) for a in ("la", "lo", "aa", "ad", "ae", "ab", "ce") for t in range(KT)]
              + ["fr0", "fr1"])


def engines(mask):
    return [1 << b for b in range(mask.bit_length()) if (mask >> b) & 1]


def spread(mask, n):
    e = engines(mask)
    e = e[::max(1, len(e) // n)][:n]
    return sum(e), len(e)


def dst(topo, c):
    rid, pid, _ = topo.addr(c)
    return DstId(rid=rid, pnc=pid)


def plan(T, topo):
    out = {}
    cores = list(T.cores)
    for c in cores:
        out.setdefault(topo.chip(c), {"ranks": []})["ranks"].append(c)
    for ch, o in out.items():
        helpers = [c for c in range(NCORES) if topo.chip(c) == ch and c not in cores]
        far = [c for c in range(NCORES) if topo.mates(topo.chip(c), ch)]
        o["mate"] = topo.chip(far[0])
        dies = sorted(set(topo.die(c) for c in helpers), reverse=True)
        a, b = [[c for c in helpers if topo.die(c) == d and topo.may_write(c, far[0])] for d in dies]
        o["out"] = [a[0], b[0], b[-1], a[-1]]
        o["in"] = sorted(set(a + b))[:NIN]
    return out


def view(buf, a, n, codes):
    v = buf[:, a:a + n]
    return v.bitcast(dt.uint8) if codes else v


def transfer(topo, src, dsts, to, mask, rsem):
    return RemoteDMATransfer(dst_ids=[dst(topo, c) for c in to], dma_engine_mask=mask,
                             remote_sem=rsem, srcs=[src], dsts=dsts)


def signal(g, topo, to, mask, rsem, lsem):
    e = engines(mask)
    g.remote_dma_fused([RemoteDMATransfer(dst_ids=[dst(topo, c)], dma_engine_mask=e[n], remote_sem=rsem)
                        for n, c in enumerate(to)], local_sem=lsem)


def rank_program(g, core, T, topo):
    chips = plan(T, topo)
    me = chips[topo.chip(core)]
    far = chips[me["mate"]]
    if T.rank_of(core) is None:
        helper_program(g, core, T, topo, me, far)
        return
    grp, pln, sem = [T.g0, T.g1], [T.p0, T.p1], T.sem
    mine = me["ranks"].index(core)
    peers = [c for c in me["ranks"] if c != core]
    own = 128 * mine
    near, nn = spread(topo.mask(core, peers[0]), KE)

    steps = product_order()
    first, last, begin, end = {}, {}, {}, {}
    for k, (p, t, i) in enumerate(steps):
        first.setdefault((p, i), k)
        last[(p, i)] = k
        begin.setdefault((p, t), k)
        end[(p, t)] = k + 1

    g.sync.dma_start(T.xb[:], T.x[:, 0:512]).then_inc(sem.xl, 16)
    for k, (p, t, i) in enumerate(steps):
        s = k % R
        n = KT * i + t
        if k - R + 1 == end[(1, LAST - 2)]:
            b = LAST % 2
            g.sync.wait_ge(sem.mm, end[(1, LAST - 2)])
            g.sync.wait_ge(sem["ab%d" % LAST], NIN * DE)
            for h, part in enumerate((T.hq0, T.hq1)):
                g.sync.dma_start(view(grp[b], HW * h, HW, True), view(part, 0, HW, True)).then_inc(sem.gl, 16)
            g.sync.dma_start(view(pln[b], 0, GW, False), view(T.hp, 0, GW, False)).then_inc(sem.gl, 16)
        if k >= R:
            g.sync.wait_ge(sem.mm, k - R + 1)
        g.sync.dma_start(view(T.wq, 128 * s, 128, True),
                         T.wc[:, 512 * n:512 * n + 512]).then_inc(sem["wl%d" % s], 16)
        g.sync.dma_start(view(T.wp, 128 * s, 128, False),
                         T.ws[:, 128 * n:128 * n + 128]).then_inc(sem["wl%d" % s], 16)

    for t in range(1, KT):
        g.scalar.wait_ge(sem.q, t)
        g.scalar.dma_start(T.xb[:], T.x[:, 512 * t:512 * t + 512]).then_inc(sem.xl, 16)

    def left(q, t):
        q.wait_ge(sem["la%d" % t], 2 * nn)
        q.wait_ge(sem["lo%d" % t], 2 * nn)

    for t in range(KT):
        s = t % 2
        if t >= 2:
            g.vector.wait_ge(sem.mm, end[(0, t - 2)])
            left(g.vector, t - 2)
        g.vector.wait_ge(sem.xl, 16 * (t + 1))
        g.vector.quantize_mx(grp[s][:, own:own + 128], pln[s][:, own:own + 128], T.xb[:]).then_inc(sem.q, 1)

    def send(t, to, rsem, lsem):
        for buf, codes in ((grp[t % 2], True), (pln[t % 2], False)):
            v = view(buf, own, 128, codes)
            g.remote_dma_fused([transfer(topo, v, [v] * len(to), to, near, rsem)], local_sem=lsem)

    for t in range(KT):
        s = t % 2
        if t >= 2:
            g.wait_ge(sem.mm, end[(0, t - 2)])
            signal(g, topo, peers, near, sem["fr%d" % s], sem.lc)
        g.wait_ge(sem.q, t + 1)
        collector = ([me["out"][t]], sem["ad%d" % t], sem["lo%d" % t])
        if t >= 2:
            send(t, *collector)
            g.wait_ge(sem["fr%d" % s], len(peers))
        send(t, peers, sem["aa%d" % t], sem["la%d" % t])
        if t < 2:
            send(t, *collector)
    for t in range(KT):
        if t < 2:
            g.wait_ge(sem.mm, end[(0, t + 2)])
            left(g, t + 2)
        elif t < LAST:
            g.wait_ge(sem.mm, end[(1, t - 2)])
        if t < LAST:
            signal(g, topo, me["in"], near, sem["ce%d" % t], sem.lc)
    g.wait_ge(sem.lc, 2 * len(peers) + LAST * NIN)

    stores = []
    count = [0] * (S + 1)
    nxt = 0
    bank_done = {}
    for p in range(2):
        for n, (c0, cw) in store_order()[p]:
            i, col = divmod(n, GR)
            if (c0, cw) == WHOLE:
                u, nxt = nxt, (nxt + 1) % S
            else:
                u = S
            j = T.rank_of((me if p == 0 else far)["ranks"][col])
            stores.append((p, i, col, j, c0, cw, u, count[u]))
            count[u] += 1
            bank_done[(p, i)] = len(stores)

    order = sorted(first, key=first.get)
    bank = {a: n % 8 for n, a in enumerate(order)}
    for k, (p, t, i) in enumerate(steps):
        s = k % R
        b = t % 2
        if k == begin[(p, t)]:
            if p == 0:
                g.tensor.wait_ge(sem.q, t + 1)
                g.tensor.wait_ge(sem["aa%d" % t], len(peers) * 2 * nn)
            elif t < LAST:
                g.tensor.wait_ge(sem["ab%d" % t], NIN * DE)
            else:
                g.tensor.wait_ge(sem.gl, 16 * 3)
        n = order.index((p, i))
        if t == 0 and n >= 8:
            g.tensor.wait_ge(sem.ev, bank_done[order[n - 8]])
        g.tensor.wait_ge(sem["wl%d" % s], 32 * (k // R + 1))
        o = 512 * bank[(p, i)]
        g.tensor.matmul_mx(T.ps[:, o:o + GW], T.wq[:, 128 * s:128 * s + 128], T.wp[:, 128 * s:128 * s + 128],
                           grp[b][:], pln[b][:], t == 0, t == KT - 1).then_inc(sem.mm, 1)

    for m, (p, i, col, j, c0, cw, u, before) in enumerate(stores):
        if before:
            g.vector.wait_ge(sem["ys%d" % u], 16 * before)
        g.vector.wait_ge(sem.mm, last[(p, i)] + 1)
        o = 512 * bank[(p, i)] + 128 * col + c0
        unit = T.yst[:, 128 * u:128 * u + cw]
        g.vector.tensor_copy(unit, T.ps[:, o:o + cw]).then_inc(sem.ev, 1)
        g.scalar.wait_ge(sem.ev, m + 1)
        o = 128 * (WT * j + i) + c0
        g.scalar.dma_start(T.y[:, o:o + cw], unit).then_inc(sem["ys%d" % u], 16)
    for u in range(S + 1):
        g.scalar.wait_ge(sem["ys%d" % u], 16 * count[u])


def helper_program(g, core, T, topo, me, far):
    grp, pln, sem = [T.g0, T.g1], [T.p0, T.p1], T.sem
    sent = 0
    ins = list(range(KT))
    ins[-2:] = [LAST, LAST - 1]
    for role, t in [("out", t) for t in range(KT)] + [("in", t) for t in ins]:
        s = t % 2
        kq, kp = T["kq%d" % t], T["kp%d" % t]
        if role == "out" and me["out"][t] == core:
            kn = spread(topo.mask(me["ranks"][0], core), KE)[1]
            g.wait_ge(sem["ad%d" % t], GR * 2 * kn)
            to = far["in"]
            e = engines(spread(topo.mask(core, to[0]), CE)[0])
            g.remote_dma_fused([transfer(topo, view(grp[s], HW * h, HW, True), [view(kq, 0, HW, True)], [to[h]],
                                         sum(e[h::2]), sem["ae%d" % t]) for h in range(2)], local_sem=sem.lx)
            g.remote_dma_fused([transfer(topo, view(pln[s], 0, GW, False), [view(kp, 0, GW, False)], [to[2]],
                                         sum(e[0::2]), sem["ae%d" % t])], local_sem=sem.lx)
            sent += len(e) + len(e[0::2])
        if role == "in" and core in me["in"]:
            h = me["in"].index(core)
            cn = spread(topo.mask(far["out"][t], core), CE)[1] // 2
            dm, dn = spread(topo.mask(core, me["ranks"][0]), DE)
            g.wait_ge(sem["ae%d" % t], cn)
            a = view(kq, 0, HW, True) if h < 2 else view(kp, 0, GW, False)
            if t == LAST:
                d = view((T.hq0, T.hq1)[h], 0, HW, True) if h < 2 else view(T.hp, 0, GW, False)
            else:
                g.wait_ge(sem["ce%d" % t], GR)
                d = view(grp[s], HW * h, HW, True) if h < 2 else view(pln[s], 0, GW, False)
            g.remote_dma_fused([transfer(topo, a, [d] * GR, me["ranks"], dm, sem["ab%d" % t])], local_sem=sem.lx)
            sent += dn
    if sent:
        g.wait_ge(sem.lx, sent)
